import numpy as np
import ml_dtypes


def mxq(x, axis, fmt="e4m3"):
    dtype, down = {"e4m3": (ml_dtypes.float8_e4m3fn, 7), "e5m2": (ml_dtypes.float8_e5m2, 14)}[fmt]
    v = np.moveaxis(np.asarray(x, np.float32).astype(ml_dtypes.bfloat16).astype(np.float64), axis, -1)
    blocks = v.reshape(v.shape[:-1] + (-1, 32))
    amax = np.abs(blocks).max(-1, keepdims=True)
    byte = np.maximum(np.where(amax > 0, np.frexp(amax)[1] - 1 + 127, 0) - down, 1)
    scale = np.exp2(byte - 127.0)
    codes = (blocks / scale).astype(np.float32).astype(dtype).astype(np.float64)
    return np.moveaxis((codes * scale).reshape(v.shape), -1, axis)


WIDE = False


def mx_kscale(k):
    if not WIDE:
        return np.ones(k)
    levels = np.array([10, -10, 5, -5, 0])
    if k % 512:
        return np.exp2(np.random.permutation(np.resize(levels, k // 32))).repeat(32)
    a = np.empty((k // 512, 16))
    for p in range(k // 512):
        a[p, :8] = np.random.permutation(np.resize(levels, 8))
        for g in range(8):
            far = levels[np.abs(levels - a[p, g]) >= 10]
            a[p, g + 8] = far[np.random.randint(len(far))]
    return np.exp2(a.ravel()).repeat(32)


BF16 = ml_dtypes.bfloat16


def bf(x):
    return np.asarray(x, np.float32).astype(BF16)


def f64(x):
    return np.asarray(x).astype(np.float64)


N, M, D, E, P = 1024, 1024, 1024, 512, 1024


def exp_kernel(a, b):
    scale = np.sqrt(a.shape[-1])
    return np.exp((mxq(a, 1, "e4m3") @ mxq(b.T, 0, "e4m3")) / scale)


def double_centre(l):
    mr = np.mean(l, axis=1)
    mc = np.mean(l, axis=0)
    mm = np.mean(mr)
    return l - mr[:, None] - mc[None, :] + mm


def draw0():
    s, g, t = mx_kscale(D), mx_kscale(E), mx_kscale(M)
    y = 0.8 * np.random.standard_normal((N, E)) + 0.3 * np.random.standard_normal((1, E))
    v = 0.8 * np.random.standard_normal((M, E)) + 0.3 * np.random.standard_normal((1, E))
    return {
        "x": bf(np.random.standard_normal((N, D)) * 0.8 * s),
        "u": bf(np.random.standard_normal((M, D)) * 0.8 / s),
        "y": bf(y * g),
        "v": bf(v / g),
        "r": bf((1.0 + 0.1 * np.random.standard_normal(M)) * t),
        "z": bf(np.random.standard_normal((M, P)) / t[:, None]),
    }


def core(x, u, y, v, r, z):
    k = exp_kernel(f64(x), f64(u))
    l = exp_kernel(f64(y), f64(v))
    lc = double_centre(l)
    a = k * lc * f64(r)[None, :]
    return (mxq(a, 1, "e4m3") @ mxq(f64(z), 0, "e4m3")) / np.sqrt(z.shape[0])


def e4m3fn_bytes(y):
    return np.clip(np.asarray(y, np.float64), -448.0, 448.0).astype(np.float32).astype(ml_dtypes.float8_e4m3fn).view(np.uint8)


def e4m3fn_values(b):
    return np.asarray(b, np.uint8).view(ml_dtypes.float8_e4m3fn).astype(np.float64)


def setup_inputs():
    d = draw0()
    x0 = np.asarray(d['z']).astype(np.float64)
    s = (np.max(np.abs(x0), axis=(1,), keepdims=True) / 448.0).astype(np.float32)
    out = {}
    for k, v in d.items():
        if k == 'z':
            out['z_bytes'] = e4m3fn_bytes(x0 / s.astype(np.float64))
            out['z_scale'] = s
        else:
            out[k] = v
    return out


def reference(x, u, y, v, r, z_bytes, z_scale):
    return core(x, u, y, v, r, e4m3fn_values(z_bytes) * z_scale.astype(np.float64))

@@ -1,0 +1,369 @@
+from contextlib import ExitStack
+
+import concourse.mybir as mybir
+from concourse.masks import make_identity
+
+N = M = D = P_OUT = 1024
+E = 512
+FLOPS = 2 * N * M * (D + E + P_OUT)
+
+F32 = mybir.dt.float32
+BF16 = mybir.dt.bfloat16
+U32 = mybir.dt.uint32
+U8 = mybir.dt.uint8
+FP8 = mybir.dt.float8_e4m3fn
+FP8X4 = mybir.dt.float8_e4m3fn_x4
+ACT = mybir.ActivationFunctionType
+ALU = mybir.AluOpType
+
+P = 128
+T = 4
+R = 512
+
+
+def tile_hsicexpkernelgrad_kernel(tc, x, u, y, v, r, z_bytes, z_scale, out):
+    nc = tc.nc
+    with ExitStack() as ctx:
+        keep = ctx.enter_context(tc.tile_pool(name="keep", bufs=1))
+        work = ctx.enter_context(tc.tile_pool(name="work", bufs=3))
+        psum = ctx.enter_context(tc.psum_pool(name="psum", bufs=6))
+        ctx.enter_context(tc.manual_schedule())
+
+        r_raw = keep.tile([P, 8], BF16, name="r_raw")
+        zs_raw = keep.tile([P, 8], F32, name="zs_raw")
+        raw = {}
+
+        def load(key, src, half, width, t0, t1):
+            if (key, half) not in raw:
+                raw[key, half] = keep.tile([P, T * width], BF16, name="raw_%s%d" % (key, half), align_bytes=64)
+            rows = src.rearrange("(h m t) k -> h m t k", m=P, t=T)
+            nc.sync.dma_start(
+                out=raw[key, half][:, t0 * width:t1 * width].rearrange("p (t k) -> p t k", k=width),
+                in_=rows[half][:, t0:t1, :],
+            )
+
+        nc.sync.dma_start(out=r_raw[:].rearrange("p (g t) -> p g t", t=T), in_=r.rearrange("(g m t) -> m g t", m=P, t=T))
+        load("v", v, 0, E, 0, 2)
+        load("v", v, 0, E, 2, 4)
+        load("y", y, 0, E, 0, 2)
+        load("y", y, 0, E, 2, 4)
+        load("v", v, 1, E, 0, 4)
+        load("y", y, 1, E, 0, 4)
+        nc.scalar.dma_start(out=zs_raw[:].rearrange("p (g t) -> p g t", t=T), in_=z_scale.rearrange("(g m t) o -> m g (t o)", m=P, t=T))
+        z_in = [keep.tile([P, T * P_OUT], U8, name="z_in%d" % g, align_bytes=64) for g in range(2)]
+        z_rows = z_bytes.rearrange("(g m t) p -> g m (t p)", m=P, t=T)
+        nc.sync.dma_start(out=z_in[0][:], in_=z_rows[0])
+        load("u", u, 0, D, 0, 2)
+        load("u", u, 0, D, 2, 4)
+        nc.sync.dma_start(out=z_in[1][:], in_=z_rows[1])
+        load("x", x, 0, D, 0, 2)
+        load("x", x, 0, D, 2, 4)
+        load("u", u, 1, D, 0, 4)
+        load("x", x, 1, D, 0, 4)
+
+        dummy = keep.tile([P, 1], F32, name="dummy")
+        nc.vector.memset(dummy[:], 1.0)
+        nc.scalar.activation(dummy[:], dummy[:], ACT.Ln)
+        ident = keep.tile([P, P], F32, name="ident")
+        make_identity(nc, ident[:])
+        mean_w = keep.tile([P, P], F32, name="mean_w")
+        nc.gpsimd.memset(mean_w[:], 1.0 / M)
+
+        r_abs = keep.tile([P, 8], F32, name="r_abs")
+        parts = keep.tile([P, 24], F32, name="parts")
+        logs = keep.tile([P, 24], F32, name="logs")
+        ln_r = keep.tile([P, 8], F32, name="ln_r")
+        sgn = keep.tile([P, 8], F32, name="sgn")
+        zs = keep.tile([P, 8], F32, name="zs")
+        nc.vector.scalar_tensor_tensor(out=r_abs[:], in0=r_raw[:], scalar=-1.0, in1=r_raw[:], op0=ALU.mult, op1=ALU.max)
+        nc.vector.tensor_scalar(out=parts[:, 0:8], in0=r_abs[:], scalar1=2.0 ** 64, scalar2=2.0 ** -62, op0=ALU.min, op1=ALU.max)
+        nc.vector.tensor_scalar(out=parts[:, 8:16], in0=r_abs[:], scalar1=2.0 ** -64, scalar2=1.0, op0=ALU.mult, op1=ALU.max)
+        nc.vector.tensor_scalar(out=parts[:, 16:24], in0=r_abs[:], scalar1=2.0 ** -62, scalar2=2.0 ** 62, op0=ALU.min, op1=ALU.mult)
+        nc.vector.tensor_scalar(out=parts[:, 16:24], in0=parts[:, 16:24], scalar1=2.0 ** -64, scalar2=None, op0=ALU.max)
+        nc.scalar.activation(logs[:], parts[:], ACT.Ln)
+        nc.scalar.activation(dummy[:], dummy[:], ACT.Exp)
+
+        def r_finish():
+            nc.gpsimd.tensor_scalar(out=sgn[:], in0=r_raw[:], scalar1=0.0, scalar2=2.0, op0=ALU.is_ge, op1=ALU.mult)
+            nc.gpsimd.tensor_scalar(out=sgn[:], in0=sgn[:], scalar1=1.0, scalar2=-1.0, op0=ALU.mult, op1=ALU.add)
+            nc.gpsimd.tensor_tensor(out=zs[:], in0=sgn[:], in1=zs_raw[:], op=ALU.mult)
+            nc.gpsimd.tensor_tensor(out=ln_r[:], in0=logs[:, 0:8], in1=logs[:, 8:16], op=ALU.add)
+            nc.gpsimd.tensor_tensor(out=ln_r[:], in0=ln_r[:], in1=logs[:, 16:24], op=ALU.add)
+
+        codes, scales, grouped, banks = {}, {}, {}, {}
+
+        def turn(key, half, g, width):
+            words = raw[key, half][:].bitcast(F32)
+            for b in range(2):
+                bank = psum.tile([P, 2, 256], F32, name="bank")
+                banks[key, half, g, b] = bank
+                for tt in range(2):
+                    for e in range(2):
+                        base = (2 * b + tt) * width // 2 + 256 * g
+                        nc.tensor.transpose(bank[:, e, P * tt:P * (tt + 1)], words[:, base + e:base + 256:2], ident[:])
+
+        def empty(key, half, g, b, eng):
+            unit = (key, half, g)
+            if b == 0:
+                grouped[unit] = work.tile([P, R * T], BF16, name="grouped", align_bytes=64, bufs=5)
+            dst = grouped[unit][:, 1024 * b:1024 * (b + 1)].bitcast(F32).rearrange("p (r e) -> p r e", e=2)
+            src = banks[key, half, g, b][:].rearrange("p e r -> p r e")
+            if eng == "V":
+                nc.vector.tensor_copy(out=dst, in_=src)
+            else:
+                nc.scalar.copy(out=dst, in_=src)
+
+        def quant(unit, src):
+            c = keep.tile([P, R], U32, name="c_%s%d%d" % unit, align_bytes=64)
+            s = keep.tile([P, R], U8, name="s_%s%d%d" % unit, align_bytes=64)
+            nc.vector.quantize_mx(out=c[:].bitcast(FP8X4), scales=s[:], in_=src)
+            codes[unit], scales[unit] = c, s
+
+        def q(key, half, g):
+            quant((key, half, g), grouped[key, half, g][:])
+
+        l_sb = keep.tile([P, 8, N], F32, name="l_sb")
+        k_sb = keep.tile([P, 8, N], F32, name="k_sb")
+        l_sums = keep.tile([P, 16], F32, name="l_sums")
+
+        def mm(stat, mov, half, h, t, passes, width=R):
+            bank = psum.tile([P, R], F32, name="bank")
+            for g in range(passes):
+                nc.tensor.matmul_mx(
+                    out=bank[:],
+                    lhsT=codes[stat, half, g][:, P * t:P * (t + 1)].bitcast(FP8X4),
+                    lhsT_scale=scales[stat, half, g][:, P * t:P * (t + 1)],
+                    rhs=codes[mov, h, g][:].bitcast(FP8X4),
+                    rhs_scale=scales[mov, h, g][:],
+                    start=(g == 0),
+                    stop=(g == passes - 1),
+                )
+            return bank
+
+        kernel_banks = {}
+
+        def l_mm(g, h):
+            for t in range(T):
+                kernel_banks["l", g, h, t] = mm("v", "y", g, h, t, 1)
+
+        def l_exp(g, h):
+            for t in range(T):
+                j = T * g + t
+                nc.scalar.activation(l_sb[:, j, R * h:R * (h + 1)], kernel_banks["l", g, h, t][:], ACT.Exp, scale=E ** -0.5, accum_out=l_sums[:, 8 * h + j:8 * h + j + 1])
+
+        def k_mm(g, h):
+            for t in range(T):
+                kernel_banks["k", g, h, t] = mm("u", "x", g, h, t, 2)
+
+        def k_exp(g, h):
+            for t in range(T):
+                j = T * g + t
+                nc.scalar.activation(k_sb[:, j, R * h:R * (h + 1)], kernel_banks["k", g, h, t][:], ACT.Exp, bias=ln_r[:, j:j + 1], scale=D ** -0.5)
+
+        pair = [work.tile([P, N], F32, name="wide32", bufs=4) for i in range(4)]
+        mr = keep.tile([P, N], F32, name="mr")
+        mm_parts = keep.tile([P, 2], F32, name="mm_parts")
+        small = keep.tile([P, 8], F32, name="small")
+        mm1 = keep.tile([P, 1], F32, name="mm1")
+        c_j = keep.tile([P, 8], F32, name="c_j")
+
+        def add_pair(i, h):
+            cols = slice(R * h, R * (h + 1))
+            nc.vector.tensor_tensor(out=pair[i][:, cols], in0=l_sb[:, 2 * i, cols], in1=l_sb[:, 2 * i + 1, cols], op=ALU.add)
+
+        def row_means_mm(h, lo, hi):
+            cols = slice(R * h, R * (h + 1))
+            terms = [pair[i][:, cols] for i in range(4)]
+            if lo == 0:
+                banks["mr", h] = psum.tile([P, R], F32, name="mr_bank", bufs=2)
+            for i in range(lo, hi):
+                nc.tensor.matmul(banks["mr", h][:], lhsT=mean_w[:], rhs=terms[i], start=(i == 0), stop=(i == len(terms) - 1))
+
+        def row_means_out(h):
+            nc.scalar.activation(mr[:, R * h:R * (h + 1)], banks["mr", h][:], ACT.Identity, accum_out=mm_parts[:, h:h + 1])
+
+        def col_sums():
+            nc.gpsimd.tensor_tensor(out=small[:], in0=l_sums[:, 0:8], in1=l_sums[:, 8:16], op=ALU.add)
+            nc.gpsimd.tensor_scalar(out=small[:], in0=small[:], scalar1=-1.0 / N, scalar2=0.0, op0=ALU.mult, op1=ALU.add)
+
+        def col_terms():
+            nc.vector.tensor_scalar(out=mm1[:], in0=mm_parts[:, 0:1], scalar1=mm_parts[:, 1:2], scalar2=1.0 / N, op0=ALU.add, op1=ALU.mult)
+            nc.vector.tensor_scalar(out=c_j[:], in0=small[:], scalar1=mm1[:], scalar2=None, op0=ALU.add)
+
+        def centre(j):
+            nc.vector.scalar_tensor_tensor(out=l_sb[:, j, :], in0=l_sb[:, j, :], scalar=c_j[:, j:j + 1], in1=mr[:], op0=ALU.add, op1=ALU.subtract)
+
+        z_wide = {}
+
+        def widen(g, t, eng):
+            if g not in z_wide:
+                z_wide[g] = work.tile([P, T, P_OUT], BF16, name="z_wide", bufs=2)
+            src = z_in[g][:, P_OUT * t:P_OUT * (t + 1)].bitcast(FP8)
+            sc = zs[:, T * g + t:T * g + t + 1]
+            if eng == "V":
+                nc.vector.tensor_scalar(out=z_wide[g][:, t, :], in0=src, scalar1=sc, scalar2=None, op0=ALU.mult)
+            else:
+                nc.scalar.activation(z_wide[g][:, t, :], src, ACT.Copy, scale=sc)
+
+        def z_group(g, n):
+            flat = work.tile([P, R * T], BF16, name="grouped", align_bytes=64, bufs=5)
+            zg = flat[:].rearrange("p (c t) -> p c t", t=T)
+            banks["zg", g, n] = flat
+            nc.vector.tensor_copy(
+                out=zg.rearrange("p (c i) t -> p c t i", i=4),
+                in_=z_wide[g][:, :, R * n:R * (n + 1)].rearrange("p t (c i) -> p c t i", i=4),
+            )
+
+        def z_quant(g, n):
+            quant(("z", n, g), banks["zg", g, n][:])
+
+        def a_make(g, h, s):
+            if s == 0:
+                banks["a", g, h] = work.tile([P, R * T], BF16, name="grouped", align_bytes=64, bufs=5)
+                codes["a", h, g] = keep.tile([P, R], U32, name="c_a%d%d" % (h, g), align_bytes=64)
+                scales["a", h, g] = keep.tile([P, R], U8, name="s_a%d%d" % (h, g), align_bytes=64)
+            w = R // 2
+            a = banks["a", g, h][:, w * T * s:w * T * (s + 1)].rearrange("p (c i t) -> p c t i", i=4, t=T)
+            cols = slice(R * h + w * s, R * h + w * (s + 1))
+            nc.vector.tensor_tensor(
+                out=a,
+                in0=l_sb[:, T * g:T * (g + 1), cols].rearrange("p t (c i) -> p c t i", i=4),
+                in1=k_sb[:, T * g:T * (g + 1), cols].rearrange("p t (c i) -> p c t i", i=4),
+                op=ALU.mult,
+            )
+
+        def a_quant(g, h, s=None):
+            lo, hi = (0, R) if s is None else (R // 2 * s, R // 2 * (s + 1))
+            nc.vector.quantize_mx(out=codes["a", h, g][:, lo:hi].bitcast(FP8X4), scales=scales["a", h, g][:, lo:hi], in_=banks["a", g, h][:, T * lo:T * hi])
+
+        out_rows = out.rearrange("(h m t) p -> h t m p", m=P, t=T)
+        staged = {}
+
+        def o_block(h, t, n, eng):
+            bank = mm("a", "z", h, n, t, 2)
+            if n == 0:
+                staged[h, t] = work.tile([P, P_OUT], F32, name="wide32", bufs=4)
+            dst = staged[h, t][:, R * n:R * (n + 1)]
+            if eng == "V":
+                nc.vector.tensor_scalar(out=dst, in0=bank[:], scalar1=M ** -0.5, scalar2=None, op0=ALU.mult)
+            else:
+                nc.scalar.activation(dst, bank[:], ACT.Copy, scale=M ** -0.5)
+            if n == 1:
+                nc.sync.dma_start(out=out_rows[h, t], in_=staged[h, t][:])
+
+        def empties(key, half, g, engs):
+            empty(key, half, g, 0, engs[0])
+            empty(key, half, g, 1, engs[1])
+
+        turn("v", 0, 0, E)
+        turn("y", 0, 0, E)
+        empties("v", 0, 0, "VV")
+        empties("y", 0, 0, "SS")
+        r_finish()
+        q("v", 0, 0)
+        q("y", 0, 0)
+        turn("v", 1, 0, E)
+        turn("y", 1, 0, E)
+        empties("v", 1, 0, "VS")
+        empties("y", 1, 0, "SS")
+        q("v", 1, 0)
+        l_mm(0, 0)
+        l_exp(0, 0)
+        widen(0, 0, "V")
+        widen(0, 1, "V")
+        q("y", 1, 0)
+        l_mm(1, 0)
+        l_exp(1, 0)
+        widen(0, 2, "V")
+        add_pair(0, 0)
+        widen(0, 3, "V")
+        add_pair(1, 0)
+        widen(1, 0, "V")
+        widen(1, 1, "V")
+        turn("u", 0, 0, D)
+        l_mm(0, 1)
+        l_exp(0, 1)
+        add_pair(2, 0)
+        add_pair(3, 0)
+        row_means_mm(0, 0, 2)
+        l_mm(1, 1)
+        l_exp(1, 1)
+        row_means_mm(0, 2, 4)
+        z_group(0, 0)
+        z_group(0, 1)
+        add_pair(0, 1)
+        z_quant(0, 0)
+        add_pair(1, 1)
+        z_quant(0, 1)
+        empties("u", 0, 0, "SS")
+        widen(1, 2, "V")
+        add_pair(2, 1)
+        widen(1, 3, "V")
+        add_pair(3, 1)
+        row_means_mm(1, 0, 4)
+        row_means_out(0)
+        z_group(1, 0)
+        z_group(1, 1)
+        z_quant(1, 0)
+        z_quant(1, 1)
+        turn("u", 0, 1, D)
+        empties("u", 0, 1, "SS")
+        col_sums()
+        row_means_out(1)
+        q("u", 0, 0)
+        col_terms()
+        q("u", 0, 1)
+        centre(0)
+        turn("x", 0, 0, D)
+        turn("x", 0, 1, D)
+        empties("x", 0, 0, "SS")
+        empties("x", 0, 1, "SS")
+        centre(1)
+        centre(2)
+        q("x", 0, 0)
+        centre(3)
+        q("x", 0, 1)
+        turn("u", 1, 0, D)
+        turn("u", 1, 1, D)
+        empties("u", 1, 0, "SS")
+        empties("u", 1, 1, "SS")
+        centre(4)
+        q("u", 1, 0)
+        centre(5)
+        q("u", 1, 1)
+        centre(6)
+        turn("x", 1, 0, D)
+        turn("x", 1, 1, D)
+        k_mm(0, 0)
+        empties("x", 1, 0, "SS")
+        k_exp(0, 0)
+        k_mm(1, 0)
+        empties("x", 1, 1, "SS")
+        k_exp(1, 0)
+        centre(7)
+        q("x", 1, 0)
+        a_make(0, 0, 0)
+        q("x", 1, 1)
+        a_make(0, 0, 1)
+        k_mm(0, 1)
+        k_exp(0, 1)
+        k_mm(1, 1)
+        k_exp(1, 1)
+        a_make(1, 0, 0)
+        a_quant(0, 0)
+        a_make(1, 0, 1)
+        a_quant(1, 0)
+        for t in range(4):
+            o_block(0, t, 0, "S")
+            o_block(0, t, 1, "S")
+        a_make(0, 1, 0)
+        a_make(1, 1, 0)
+        a_quant(0, 1, 0)
+        a_make(0, 1, 1)
+        a_quant(1, 1, 0)
+        a_make(1, 1, 1)
+        a_quant(0, 1, 1)
+        a_quant(1, 1, 1)
+        for t in range(4):
+            o_block(1, t, 0, "S")
+            o_block(1, t, 1, "S" if t < 2 else "V")

@@ -42,7 +42,7 @@ def tile_hsicexpkernelgrad_kernel(tc, x, u, y, v, r, z_bytes, z_scale, out):
                 in_=rows[half][:, t0:t1, :],
             )
 
-        nc.sync.dma_start(out=r_raw[:].rearrange("p (g t) -> p g t", t=T), in_=r.rearrange("(g m t) -> m g t", m=P, t=T))
+        nc.scalar.dma_start(out=r_raw[:].rearrange("p (g t) -> p g t", t=T), in_=r.rearrange("(g m t) -> m g t", m=P, t=T))
         load("v", v, 0, E, 0, 2)
         load("v", v, 0, E, 2, 4)
         load("y", y, 0, E, 0, 2)
@@ -92,22 +92,27 @@ def tile_hsicexpkernelgrad_kernel(tc, x, u, y, v, r, z_bytes, z_scale, out):
 
         codes, scales, grouped, banks = {}, {}, {}, {}
 
-        def turn(key, half, g, width):
+        width_of = {"v": E, "y": E, "u": D, "x": D}
+
+        def new_bank(b):
+            return psum.tile([P, R], F32, name="bank", tag="bank%d" % b, bufs=1)
+
+        def turn(key, half, g, b, slot):
             words = raw[key, half][:].bitcast(F32)
-            for b in range(2):
-                bank = psum.tile([P, 2, 256], F32, name="bank")
-                banks[key, half, g, b] = bank
-                for tt in range(2):
-                    for e in range(2):
-                        base = (2 * b + tt) * width // 2 + 256 * g
-                        nc.tensor.transpose(bank[:, e, P * tt:P * (tt + 1)], words[:, base + e:base + 256:2], ident[:])
+            bank = new_bank(slot)
+            banks[key, half, g, b] = bank
+            for tt in range(2):
+                for e in range(2):
+                    base = (2 * b + tt) * width_of[key] // 2 + 256 * g
+                    to = 256 * e + P * tt
+                    nc.tensor.transpose(bank[:, to:to + P], words[:, base + e:base + 256:2], ident[:])
 
         def empty(key, half, g, b, eng):
             unit = (key, half, g)
-            if b == 0:
-                grouped[unit] = work.tile([P, R * T], BF16, name="grouped", align_bytes=64, bufs=5)
+            if unit not in grouped:
+                grouped[unit] = work.tile([P, R * T], BF16, name="grouped", align_bytes=64, bufs=8)
             dst = grouped[unit][:, 1024 * b:1024 * (b + 1)].bitcast(F32).rearrange("p (r e) -> p r e", e=2)
-            src = banks[key, half, g, b][:].rearrange("p e r -> p r e")
+            src = banks[key, half, g, b][:].rearrange("p (e r) -> p r e", e=2)
             if eng == "V":
                 nc.vector.tensor_copy(out=dst, in_=src)
             else:
@@ -123,11 +128,11 @@ def tile_hsicexpkernelgrad_kernel(tc, x, u, y, v, r, z_bytes, z_scale, out):
             quant((key, half, g), grouped[key, half, g][:])
 
         l_sb = keep.tile([P, 8, N], F32, name="l_sb")
-        k_sb = keep.tile([P, 8, N], F32, name="k_sb")
+        k_sb = {}
         l_sums = keep.tile([P, 16], F32, name="l_sums")
 
-        def mm(stat, mov, half, h, t, passes, width=R):
-            bank = psum.tile([P, R], F32, name="bank")
+        def mm(stat, mov, half, h, t, passes, slot):
+            bank = new_bank(slot)
             for g in range(passes):
                 nc.tensor.matmul_mx(
                     out=bank[:],
@@ -142,23 +147,22 @@ def tile_hsicexpkernelgrad_kernel(tc, x, u, y, v, r, z_bytes, z_scale, out):
 
         kernel_banks = {}
 
-        def l_mm(g, h):
-            for t in range(T):
-                kernel_banks["l", g, h, t] = mm("v", "y", g, h, t, 1)
+        kernel_banks = {}
 
-        def l_exp(g, h):
-            for t in range(T):
-                j = T * g + t
-                nc.scalar.activation(l_sb[:, j, R * h:R * (h + 1)], kernel_banks["l", g, h, t][:], ACT.Exp, scale=E ** -0.5, accum_out=l_sums[:, 8 * h + j:8 * h + j + 1])
+        def l_mm(j, h, slot):
+            kernel_banks["l", j, h] = mm("v", "y", j // T, h, j % T, 1, slot)
 
-        def k_mm(g, h):
-            for t in range(T):
-                kernel_banks["k", g, h, t] = mm("u", "x", g, h, t, 2)
+        def l_exp(j, h):
+            nc.scalar.activation(l_sb[:, j, R * h:R * (h + 1)], kernel_banks["l", j, h][:], ACT.Exp, scale=E ** -0.5, accum_out=l_sums[:, 8 * h + j:8 * h + j + 1])
 
-        def k_exp(g, h):
-            for t in range(T):
-                j = T * g + t
-                nc.scalar.activation(k_sb[:, j, R * h:R * (h + 1)], kernel_banks["k", g, h, t][:], ACT.Exp, bias=ln_r[:, j:j + 1], scale=D ** -0.5)
+        def k_mm(j, h, slot):
+            kernel_banks["k", j, h] = mm("u", "x", j // T, h, j % T, 2, slot)
+
+        def k_exp(j, h):
+            g = j // T
+            if g not in k_sb:
+                k_sb[g] = work.tile([P, T, N], F32, name="k_sb", tag="late%d" % g, bufs=1)
+            nc.scalar.activation(k_sb[g][:, j % T, R * h:R * (h + 1)], kernel_banks["k", j, h][:], ACT.Exp, bias=ln_r[:, j:j + 1], scale=D ** -0.5)
 
         pair = [work.tile([P, N], F32, name="wide32", bufs=4) for i in range(4)]
         mr = keep.tile([P, N], F32, name="mr")
@@ -171,13 +175,10 @@ def tile_hsicexpkernelgrad_kernel(tc, x, u, y, v, r, z_bytes, z_scale, out):
             cols = slice(R * h, R * (h + 1))
             nc.vector.tensor_tensor(out=pair[i][:, cols], in0=l_sb[:, 2 * i, cols], in1=l_sb[:, 2 * i + 1, cols], op=ALU.add)
 
-        def row_means_mm(h, lo, hi):
-            cols = slice(R * h, R * (h + 1))
-            terms = [pair[i][:, cols] for i in range(4)]
-            if lo == 0:
-                banks["mr", h] = psum.tile([P, R], F32, name="mr_bank", bufs=2)
-            for i in range(lo, hi):
-                nc.tensor.matmul(banks["mr", h][:], lhsT=mean_w[:], rhs=terms[i], start=(i == 0), stop=(i == len(terms) - 1))
+        def row_means_mm(i, h, n):
+            if n == 0:
+                banks["mr", h] = new_bank(6 + h)
+            nc.tensor.matmul(banks["mr", h][:], lhsT=mean_w[:], rhs=pair[i][:, R * h:R * (h + 1)], start=(n == 0), stop=(n == 3))
 
         def row_means_out(h):
             nc.scalar.activation(mr[:, R * h:R * (h + 1)], banks["mr", h][:], ACT.Identity, accum_out=mm_parts[:, h:h + 1])
@@ -197,7 +198,7 @@ def tile_hsicexpkernelgrad_kernel(tc, x, u, y, v, r, z_bytes, z_scale, out):
 
         def widen(g, t, eng):
             if g not in z_wide:
-                z_wide[g] = work.tile([P, T, P_OUT], BF16, name="z_wide", bufs=2)
+                z_wide[g] = work.tile([P, T, P_OUT], BF16, name="z_wide", tag="late%d" % g, bufs=1)
             src = z_in[g][:, P_OUT * t:P_OUT * (t + 1)].bitcast(FP8)
             sc = zs[:, T * g + t:T * g + t + 1]
             if eng == "V":
@@ -206,7 +207,7 @@ def tile_hsicexpkernelgrad_kernel(tc, x, u, y, v, r, z_bytes, z_scale, out):
                 nc.scalar.activation(z_wide[g][:, t, :], src, ACT.Copy, scale=sc)
 
         def z_group(g, n):
-            flat = work.tile([P, R * T], BF16, name="grouped", align_bytes=64, bufs=5)
+            flat = work.tile([P, R * T], BF16, name="zg", align_bytes=64, bufs=2)
             zg = flat[:].rearrange("p (c t) -> p c t", t=T)
             banks["zg", g, n] = flat
             nc.vector.tensor_copy(
@@ -217,153 +218,268 @@ def tile_hsicexpkernelgrad_kernel(tc, x, u, y, v, r, z_bytes, z_scale, out):
         def z_quant(g, n):
             quant(("z", n, g), banks["zg", g, n][:])
 
-        def a_make(g, h, s):
-            if s == 0:
-                banks["a", g, h] = work.tile([P, R * T], BF16, name="grouped", align_bytes=64, bufs=5)
+        def a_make(g, lo, hi):
+            h, w = lo // R, hi - lo
+            if (h, g) not in grouped:
+                grouped[h, g] = work.tile([P, R * T], BF16, name="grouped", align_bytes=64, bufs=8)
                 codes["a", h, g] = keep.tile([P, R], U32, name="c_a%d%d" % (h, g), align_bytes=64)
                 scales["a", h, g] = keep.tile([P, R], U8, name="s_a%d%d" % (h, g), align_bytes=64)
-            w = R // 2
-            a = banks["a", g, h][:, w * T * s:w * T * (s + 1)].rearrange("p (c i t) -> p c t i", i=4, t=T)
-            cols = slice(R * h + w * s, R * h + w * (s + 1))
+            at = lo - R * h
             nc.vector.tensor_tensor(
-                out=a,
-                in0=l_sb[:, T * g:T * (g + 1), cols].rearrange("p t (c i) -> p c t i", i=4),
-                in1=k_sb[:, T * g:T * (g + 1), cols].rearrange("p t (c i) -> p c t i", i=4),
+                out=grouped[h, g][:, T * at:T * (at + w)].rearrange("p (c i t) -> p c t i", i=4, t=T),
+                in0=l_sb[:, T * g:T * (g + 1), lo:hi].rearrange("p t (c i) -> p c t i", i=4),
+                in1=k_sb[g][:, :, lo:hi].rearrange("p t (c i) -> p c t i", i=4),
                 op=ALU.mult,
             )
 
-        def a_quant(g, h, s=None):
-            lo, hi = (0, R) if s is None else (R // 2 * s, R // 2 * (s + 1))
-            nc.vector.quantize_mx(out=codes["a", h, g][:, lo:hi].bitcast(FP8X4), scales=scales["a", h, g][:, lo:hi], in_=banks["a", g, h][:, T * lo:T * hi])
+        def a_quant(g, lo, hi):
+            h = lo // R
+            at, to = lo - R * h, hi - R * h
+            nc.vector.quantize_mx(out=codes["a", h, g][:, at:to].bitcast(FP8X4), scales=scales["a", h, g][:, at:to], in_=grouped[h, g][:, T * at:T * to])
 
         out_rows = out.rearrange("(h m t) p -> h t m p", m=P, t=T)
         staged = {}
 
-        def o_block(h, t, n, eng):
-            bank = mm("a", "z", h, n, t, 2)
-            if n == 0:
-                staged[h, t] = work.tile([P, P_OUT], F32, name="wide32", bufs=4)
-            dst = staged[h, t][:, R * n:R * (n + 1)]
+        def o_mm(tile, n, slot):
+            banks["o", tile, n] = mm("a", "z", tile // T, n, tile % T, 2, slot)
+
+        def o_out(tile, n, eng):
+            bank = banks["o", tile, n]
+            if tile not in staged:
+                staged[tile] = work.tile([P, P_OUT], F32, name="wide32", bufs=4)
+                count[tile] = 0
+            cols = slice(R * n, R * (n + 1))
+            dst = staged[tile][:, cols]
             if eng == "V":
                 nc.vector.tensor_scalar(out=dst, in0=bank[:], scalar1=M ** -0.5, scalar2=None, op0=ALU.mult)
             else:
                 nc.scalar.activation(dst, bank[:], ACT.Copy, scale=M ** -0.5)
-            if n == 1:
-                nc.sync.dma_start(out=out_rows[h, t], in_=staged[h, t][:])
+            count[tile] += 1
+            if tile >= 6:
+                nc.sync.dma_start(out=out_rows[tile // T, tile % T][:, cols], in_=dst)
+            elif count[tile] == 2:
+                nc.sync.dma_start(out=out_rows[tile // T, tile % T], in_=staged[tile][:])
 
-        def empties(key, half, g, engs):
-            empty(key, half, g, 0, engs[0])
-            empty(key, half, g, 1, engs[1])
+        count = {}
 
-        turn("v", 0, 0, E)
-        turn("y", 0, 0, E)
-        empties("v", 0, 0, "VV")
-        empties("y", 0, 0, "SS")
         r_finish()
+        turn("v", 0, 0, 0, 0)
+        turn("v", 0, 0, 1, 1)
+        empty("v", 0, 0, 0, "V")
+        turn("y", 0, 0, 0, 2)
+        empty("v", 0, 0, 1, "V")
+        turn("y", 0, 0, 1, 3)
+        empty("y", 0, 0, 0, "S")
         q("v", 0, 0)
+        empty("y", 0, 0, 1, "S")
+        turn("v", 1, 0, 0, 4)
+        turn("v", 1, 0, 1, 5)
         q("y", 0, 0)
-        turn("v", 1, 0, E)
-        turn("y", 1, 0, E)
-        empties("v", 1, 0, "VS")
-        empties("y", 1, 0, "SS")
+        empty("v", 1, 0, 0, "S")
+        turn("y", 1, 0, 0, 0)
+        empty("v", 1, 0, 1, "V")
+        turn("y", 1, 0, 1, 1)
+        empty("y", 1, 0, 0, "S")
+        widen(0, 2, "V")
+        l_mm(2, 0, 2)
+        empty("y", 1, 0, 1, "S")
+        l_mm(3, 0, 3)
         q("v", 1, 0)
-        l_mm(0, 0)
+        l_mm(0, 0, 4)
+        l_exp(2, 0)
+        l_mm(1, 0, 5)
+        q("y", 1, 0)
+        turn("u", 0, 1, 0, 0)
         l_exp(0, 0)
         widen(0, 0, "V")
-        widen(0, 1, "V")
-        q("y", 1, 0)
-        l_mm(1, 0)
+        l_mm(6, 0, 1)
         l_exp(1, 0)
-        widen(0, 2, "V")
-        add_pair(0, 0)
+        l_mm(0, 1, 2)
         widen(0, 3, "V")
-        add_pair(1, 0)
-        widen(1, 0, "V")
-        widen(1, 1, "V")
-        turn("u", 0, 0, D)
-        l_mm(0, 1)
+        l_mm(1, 1, 4)
+        l_exp(3, 0)
+        l_mm(2, 1, 5)
+        add_pair(0, 0)
         l_exp(0, 1)
-        add_pair(2, 0)
-        add_pair(3, 0)
-        row_means_mm(0, 0, 2)
-        l_mm(1, 1)
-        l_exp(1, 1)
-        row_means_mm(0, 2, 4)
-        z_group(0, 0)
-        z_group(0, 1)
-        add_pair(0, 1)
-        z_quant(0, 0)
-        add_pair(1, 1)
-        z_quant(0, 1)
-        empties("u", 0, 0, "SS")
+        l_mm(3, 1, 3)
         widen(1, 2, "V")
-        add_pair(2, 1)
+        row_means_mm(0, 0, 0)
+        l_exp(2, 1)
         widen(1, 3, "V")
-        add_pair(3, 1)
-        row_means_mm(1, 0, 4)
-        row_means_out(0)
+        l_exp(3, 1)
+        add_pair(1, 0)
+        l_mm(7, 0, 2)
+        l_exp(1, 1)
+        l_mm(4, 1, 5)
+        widen(1, 0, "V")
+        l_mm(5, 1, 3)
+        widen(1, 1, "S")
+        row_means_mm(1, 0, 1)
+        add_pair(0, 1)
+        add_pair(1, 1)
+        l_exp(4, 1)
+        row_means_mm(0, 1, 0)
         z_group(1, 0)
-        z_group(1, 1)
+        l_exp(5, 1)
+        l_exp(6, 0)
+        l_mm(4, 0, 4)
+        add_pair(2, 1)
+        l_mm(5, 0, 5)
+        l_exp(7, 0)
+        l_mm(6, 1, 3)
         z_quant(1, 0)
-        z_quant(1, 1)
-        turn("u", 0, 1, D)
-        empties("u", 0, 1, "SS")
+        l_mm(7, 1, 1)
+        row_means_mm(1, 1, 1)
+        l_exp(6, 1)
+        add_pair(3, 0)
+        l_exp(7, 1)
+        z_group(1, 1)
+        row_means_mm(2, 1, 2)
+        l_exp(4, 0)
+        l_exp(5, 0)
         col_sums()
+        add_pair(3, 1)
+        turn("u", 0, 1, 1, 2)
+        widen(0, 1, "S")
+        z_quant(1, 1)
+        row_means_mm(3, 1, 3)
+        add_pair(2, 0)
+        empty("u", 0, 1, 1, "S")
+        z_group(0, 0)
+        row_means_mm(2, 0, 2)
+        empty("u", 0, 1, 0, "S")
         row_means_out(1)
-        q("u", 0, 0)
-        col_terms()
         q("u", 0, 1)
-        centre(0)
-        turn("x", 0, 0, D)
-        turn("x", 0, 1, D)
-        empties("x", 0, 0, "SS")
-        empties("x", 0, 1, "SS")
-        centre(1)
-        centre(2)
-        q("x", 0, 0)
-        centre(3)
-        q("x", 0, 1)
-        turn("u", 1, 0, D)
-        turn("u", 1, 1, D)
-        empties("u", 1, 0, "SS")
-        empties("u", 1, 1, "SS")
-        centre(4)
-        q("u", 1, 0)
-        centre(5)
-        q("u", 1, 1)
-        centre(6)
-        turn("x", 1, 0, D)
-        turn("x", 1, 1, D)
-        k_mm(0, 0)
-        empties("x", 1, 0, "SS")
-        k_exp(0, 0)
-        k_mm(1, 0)
-        empties("x", 1, 1, "SS")
-        k_exp(1, 0)
+        row_means_mm(3, 0, 3)
+        z_quant(0, 0)
+        z_group(0, 1)
+        turn("x", 1, 1, 0, 3)
+        row_means_out(0)
+        turn("x", 1, 1, 1, 1)
+        empty("x", 1, 1, 0, "S")
+        col_terms()
+        turn("x", 0, 1, 0, 4)
+        z_quant(0, 1)
+        empty("x", 1, 1, 1, "S")
+        turn("x", 0, 1, 1, 5)
         centre(7)
-        q("x", 1, 0)
-        a_make(0, 0, 0)
+        empty("x", 0, 1, 0, "S")
+        turn("x", 0, 0, 0, 2)
+        empty("x", 0, 1, 1, "S")
+        turn("x", 0, 0, 1, 0)
+        centre(4)
+        empty("x", 0, 0, 0, "S")
+        turn("u", 1, 1, 0, 3)
+        empty("x", 0, 0, 1, "S")
+        turn("u", 1, 1, 1, 1)
         q("x", 1, 1)
-        a_make(0, 0, 1)
-        k_mm(0, 1)
+        empty("u", 1, 1, 0, "S")
+        turn("u", 0, 0, 0, 4)
+        turn("u", 0, 0, 1, 5)
+        q("x", 0, 0)
+        empty("u", 1, 1, 1, "S")
+        turn("x", 1, 0, 0, 2)
+        empty("u", 0, 0, 0, "S")
+        q("x", 0, 1)
+        turn("x", 1, 0, 1, 0)
+        empty("u", 0, 0, 1, "S")
+        q("u", 1, 1)
+        turn("u", 1, 0, 0, 3)
+        empty("x", 1, 0, 0, "S")
+        q("u", 0, 0)
+        turn("u", 1, 0, 1, 1)
+        empty("x", 1, 0, 1, "S")
+        centre(5)
+        k_mm(0, 0, 4)
+        empty("u", 1, 0, 1, "S")
+        k_mm(1, 0, 5)
+        empty("u", 1, 0, 0, "S")
+        q("x", 1, 0)
+        k_mm(2, 0, 2)
+        k_exp(0, 0)
+        q("u", 1, 0)
+        k_mm(3, 0, 0)
+        k_exp(1, 0)
+        centre(3)
+        k_mm(0, 1, 1)
+        k_exp(2, 0)
+        k_mm(4, 0, 3)
+        k_exp(3, 0)
+        centre(1)
+        k_mm(5, 0, 4)
+        k_exp(4, 0)
+        k_mm(1, 1, 5)
+        k_exp(5, 0)
+        k_mm(6, 0, 2)
+        centre(6)
         k_exp(0, 1)
-        k_mm(1, 1)
+        k_mm(7, 0, 0)
+        k_exp(6, 0)
+        k_mm(4, 1, 3)
+        centre(0)
+        k_exp(7, 0)
+        k_mm(5, 1, 4)
         k_exp(1, 1)
-        a_make(1, 0, 0)
-        a_quant(0, 0)
-        a_make(1, 0, 1)
-        a_quant(1, 0)
-        for t in range(4):
-            o_block(0, t, 0, "S")
-            o_block(0, t, 1, "S")
-        a_make(0, 1, 0)
-        a_make(1, 1, 0)
-        a_quant(0, 1, 0)
-        a_make(0, 1, 1)
-        a_quant(1, 1, 0)
-        a_make(1, 1, 1)
-        a_quant(0, 1, 1)
-        a_quant(1, 1, 1)
-        for t in range(4):
-            o_block(1, t, 0, "S")
-            o_block(1, t, 1, "S" if t < 2 else "V")
+        k_mm(6, 1, 1)
+        centre(2)
+        k_mm(7, 1, 2)
+        k_exp(4, 1)
+        k_mm(2, 1, 0)
+        k_exp(6, 1)
+        a_make(1, 256, 512)
+        k_mm(3, 1, 5)
+        k_exp(7, 1)
+        k_exp(2, 1)
+        a_make(0, 256, 512)
+        k_exp(3, 1)
+        k_exp(5, 1)
+        a_quant(1, 256, 512)
+        a_quant(0, 256, 512)
+        a_make(1, 896, 1024)
+        o_mm(2, 0, 3)
+        a_make(0, 896, 1024)
+        o_mm(2, 1, 1)
+        o_out(2, 0, "S")
+        a_quant(1, 896, 1024)
+        o_mm(3, 0, 2)
+        a_make(0, 0, 256)
+        o_out(2, 1, "S")
+        o_mm(3, 1, 0)
+        o_out(3, 0, "S")
+        a_quant(0, 896, 1024)
+        o_out(3, 1, "S")
+        a_make(1, 0, 256)
+        o_mm(7, 0, 5)
+        o_mm(7, 1, 4)
+        o_out(7, 0, "S")
+        a_quant(0, 0, 256)
+        a_quant(1, 0, 256)
+        o_out(7, 1, "S")
+        a_make(0, 512, 768)
+        o_mm(1, 0, 3)
+        o_mm(1, 1, 1)
+        o_out(1, 0, "S")
+        a_make(1, 512, 768)
+        o_mm(0, 0, 2)
+        o_out(1, 1, "S")
+        o_mm(0, 1, 0)
+        o_out(0, 0, "S")
+        a_quant(0, 512, 768)
+        a_quant(1, 512, 768)
+        o_out(0, 1, "S")
+        a_make(1, 768, 896)
+        o_mm(5, 0, 5)
+        a_make(0, 768, 896)
+        o_mm(5, 1, 4)
+        o_out(5, 0, "S")
+        a_quant(1, 768, 896)
+        o_mm(4, 0, 3)
+        a_quant(0, 768, 896)
+        o_out(5, 1, "S")
+        o_mm(4, 1, 1)
+        o_out(4, 0, "S")
+        o_mm(6, 0, 2)
+        o_out(4, 1, "V")
+        o_mm(6, 1, 0)
+        o_out(6, 0, "V")
+        o_out(6, 1, "S")

from contextlib import ExitStack

import concourse.mybir as mybir
from concourse.masks import make_identity

N = M = D = P_OUT = 1024
E = 512
FLOPS = 2 * N * M * (D + E + P_OUT)

F32 = mybir.dt.float32
BF16 = mybir.dt.bfloat16
U32 = mybir.dt.uint32
U8 = mybir.dt.uint8
FP8 = mybir.dt.float8_e4m3fn
FP8X4 = mybir.dt.float8_e4m3fn_x4
ACT = mybir.ActivationFunctionType
ALU = mybir.AluOpType

P = 128
T = 4
R = 512


def tile_hsicexpkernelgrad_kernel(tc, x, u, y, v, r, z_bytes, z_scale, out):
    nc = tc.nc
    with ExitStack() as ctx:
        keep = ctx.enter_context(tc.tile_pool(name="keep", bufs=1))
        work = ctx.enter_context(tc.tile_pool(name="work", bufs=3))
        psum = ctx.enter_context(tc.psum_pool(name="psum", bufs=6))
        ctx.enter_context(tc.manual_schedule())

        r_raw = keep.tile([P, 8], BF16, name="r_raw")
        zs_raw = keep.tile([P, 8], F32, name="zs_raw")
        raw = {}

        def load(key, src, half, width, t0, t1):
            if (key, half) not in raw:
                raw[key, half] = keep.tile([P, T * width], BF16, name="raw_%s%d" % (key, half), align_bytes=64)
            rows = src.rearrange("(h m t) k -> h m t k", m=P, t=T)
            nc.sync.dma_start(
                out=raw[key, half][:, t0 * width:t1 * width].rearrange("p (t k) -> p t k", k=width),
                in_=rows[half][:, t0:t1, :],
            )

        nc.scalar.dma_start(out=r_raw[:].rearrange("p (g t) -> p g t", t=T), in_=r.rearrange("(g m t) -> m g t", m=P, t=T))
        load("v", v, 0, E, 0, 2)
        load("v", v, 0, E, 2, 4)
        load("y", y, 0, E, 0, 2)
        load("y", y, 0, E, 2, 4)
        load("v", v, 1, E, 0, 4)
        load("y", y, 1, E, 0, 4)
        nc.scalar.dma_start(out=zs_raw[:].rearrange("p (g t) -> p g t", t=T), in_=z_scale.rearrange("(g m t) o -> m g (t o)", m=P, t=T))
        z_in = [keep.tile([P, T * P_OUT], U8, name="z_in%d" % g, align_bytes=64) for g in range(2)]
        z_rows = z_bytes.rearrange("(g m t) p -> g m (t p)", m=P, t=T)
        nc.sync.dma_start(out=z_in[0][:], in_=z_rows[0])
        load("u", u, 0, D, 0, 2)
        load("u", u, 0, D, 2, 4)
        nc.sync.dma_start(out=z_in[1][:], in_=z_rows[1])
        load("x", x, 0, D, 0, 2)
        load("x", x, 0, D, 2, 4)
        load("u", u, 1, D, 0, 4)
        load("x", x, 1, D, 0, 4)

        dummy = keep.tile([P, 1], F32, name="dummy")
        nc.vector.memset(dummy[:], 1.0)
        nc.scalar.activation(dummy[:], dummy[:], ACT.Ln)
        ident = keep.tile([P, P], F32, name="ident")
        make_identity(nc, ident[:])
        mean_w = keep.tile([P, P], F32, name="mean_w")
        nc.gpsimd.memset(mean_w[:], 1.0 / M)

        r_abs = keep.tile([P, 8], F32, name="r_abs")
        parts = keep.tile([P, 24], F32, name="parts")
        logs = keep.tile([P, 24], F32, name="logs")
        ln_r = keep.tile([P, 8], F32, name="ln_r")
        sgn = keep.tile([P, 8], F32, name="sgn")
        zs = keep.tile([P, 8], F32, name="zs")
        nc.vector.scalar_tensor_tensor(out=r_abs[:], in0=r_raw[:], scalar=-1.0, in1=r_raw[:], op0=ALU.mult, op1=ALU.max)
        nc.vector.tensor_scalar(out=parts[:, 0:8], in0=r_abs[:], scalar1=2.0 ** 64, scalar2=2.0 ** -62, op0=ALU.min, op1=ALU.max)
        nc.vector.tensor_scalar(out=parts[:, 8:16], in0=r_abs[:], scalar1=2.0 ** -64, scalar2=1.0, op0=ALU.mult, op1=ALU.max)
        nc.vector.tensor_scalar(out=parts[:, 16:24], in0=r_abs[:], scalar1=2.0 ** -62, scalar2=2.0 ** 62, op0=ALU.min, op1=ALU.mult)
        nc.vector.tensor_scalar(out=parts[:, 16:24], in0=parts[:, 16:24], scalar1=2.0 ** -64, scalar2=None, op0=ALU.max)
        nc.scalar.activation(logs[:], parts[:], ACT.Ln)
        nc.scalar.activation(dummy[:], dummy[:], ACT.Exp)

        def r_finish():
            nc.gpsimd.tensor_scalar(out=sgn[:], in0=r_raw[:], scalar1=0.0, scalar2=2.0, op0=ALU.is_ge, op1=ALU.mult)
            nc.gpsimd.tensor_scalar(out=sgn[:], in0=sgn[:], scalar1=1.0, scalar2=-1.0, op0=ALU.mult, op1=ALU.add)
            nc.gpsimd.tensor_tensor(out=zs[:], in0=sgn[:], in1=zs_raw[:], op=ALU.mult)
            nc.gpsimd.tensor_tensor(out=ln_r[:], in0=logs[:, 0:8], in1=logs[:, 8:16], op=ALU.add)
            nc.gpsimd.tensor_tensor(out=ln_r[:], in0=ln_r[:], in1=logs[:, 16:24], op=ALU.add)

        codes, scales, grouped, banks = {}, {}, {}, {}

        width_of = {"v": E, "y": E, "u": D, "x": D}

        def new_bank(b):
            return psum.tile([P, R], F32, name="bank", tag="bank%d" % b, bufs=1)

        def turn(key, half, g, b, slot):
            words = raw[key, half][:].bitcast(F32)
            bank = new_bank(slot)
            banks[key, half, g, b] = bank
            for tt in range(2):
                for e in range(2):
                    base = (2 * b + tt) * width_of[key] // 2 + 256 * g
                    to = 256 * e + P * tt
                    nc.tensor.transpose(bank[:, to:to + P], words[:, base + e:base + 256:2], ident[:])

        def empty(key, half, g, b, eng):
            unit = (key, half, g)
            if unit not in grouped:
                grouped[unit] = work.tile([P, R * T], BF16, name="grouped", align_bytes=64, bufs=8)
            dst = grouped[unit][:, 1024 * b:1024 * (b + 1)].bitcast(F32).rearrange("p (r e) -> p r e", e=2)
            src = banks[key, half, g, b][:].rearrange("p (e r) -> p r e", e=2)
            if eng == "V":
                nc.vector.tensor_copy(out=dst, in_=src)
            else:
                nc.scalar.copy(out=dst, in_=src)

        def quant(unit, src):
            c = keep.tile([P, R], U32, name="c_%s%d%d" % unit, align_bytes=64)
            s = keep.tile([P, R], U8, name="s_%s%d%d" % unit, align_bytes=64)
            nc.vector.quantize_mx(out=c[:].bitcast(FP8X4), scales=s[:], in_=src)
            codes[unit], scales[unit] = c, s

        def q(key, half, g):
            quant((key, half, g), grouped[key, half, g][:])

        l_sb = keep.tile([P, 8, N], F32, name="l_sb")
        k_sb = {}
        l_sums = keep.tile([P, 16], F32, name="l_sums")

        def mm(stat, mov, half, h, t, passes, slot):
            bank = new_bank(slot)
            for g in range(passes):
                nc.tensor.matmul_mx(
                    out=bank[:],
                    lhsT=codes[stat, half, g][:, P * t:P * (t + 1)].bitcast(FP8X4),
                    lhsT_scale=scales[stat, half, g][:, P * t:P * (t + 1)],
                    rhs=codes[mov, h, g][:].bitcast(FP8X4),
                    rhs_scale=scales[mov, h, g][:],
                    start=(g == 0),
                    stop=(g == passes - 1),
                )
            return bank

        kernel_banks = {}

        kernel_banks = {}

        def l_mm(j, h, slot):
            kernel_banks["l", j, h] = mm("v", "y", j // T, h, j % T, 1, slot)

        def l_exp(j, h):
            nc.scalar.activation(l_sb[:, j, R * h:R * (h + 1)], kernel_banks["l", j, h][:], ACT.Exp, scale=E ** -0.5, accum_out=l_sums[:, 8 * h + j:8 * h + j + 1])

        def k_mm(j, h, slot):
            kernel_banks["k", j, h] = mm("u", "x", j // T, h, j % T, 2, slot)

        def k_exp(j, h):
            g = j // T
            if g not in k_sb:
                k_sb[g] = work.tile([P, T, N], F32, name="k_sb", tag="late%d" % g, bufs=1)
            nc.scalar.activation(k_sb[g][:, j % T, R * h:R * (h + 1)], kernel_banks["k", j, h][:], ACT.Exp, bias=ln_r[:, j:j + 1], scale=D ** -0.5)

        pair = [work.tile([P, N], F32, name="wide32", bufs=4) for i in range(4)]
        mr = keep.tile([P, N], F32, name="mr")
        mm_parts = keep.tile([P, 2], F32, name="mm_parts")
        small = keep.tile([P, 8], F32, name="small")
        mm1 = keep.tile([P, 1], F32, name="mm1")
        c_j = keep.tile([P, 8], F32, name="c_j")

        def add_pair(i, h):
            cols = slice(R * h, R * (h + 1))
            nc.vector.tensor_tensor(out=pair[i][:, cols], in0=l_sb[:, 2 * i, cols], in1=l_sb[:, 2 * i + 1, cols], op=ALU.add)

        def row_means_mm(i, h, n):
            if n == 0:
                banks["mr", h] = new_bank(6 + h)
            nc.tensor.matmul(banks["mr", h][:], lhsT=mean_w[:], rhs=pair[i][:, R * h:R * (h + 1)], start=(n == 0), stop=(n == 3))

        def row_means_out(h):
            nc.scalar.activation(mr[:, R * h:R * (h + 1)], banks["mr", h][:], ACT.Identity, accum_out=mm_parts[:, h:h + 1])

        def col_sums():
            nc.gpsimd.tensor_tensor(out=small[:], in0=l_sums[:, 0:8], in1=l_sums[:, 8:16], op=ALU.add)
            nc.gpsimd.tensor_scalar(out=small[:], in0=small[:], scalar1=-1.0 / N, scalar2=0.0, op0=ALU.mult, op1=ALU.add)

        def col_terms():
            nc.vector.tensor_scalar(out=mm1[:], in0=mm_parts[:, 0:1], scalar1=mm_parts[:, 1:2], scalar2=1.0 / N, op0=ALU.add, op1=ALU.mult)
            nc.vector.tensor_scalar(out=c_j[:], in0=small[:], scalar1=mm1[:], scalar2=None, op0=ALU.add)

        def centre(j):
            nc.vector.scalar_tensor_tensor(out=l_sb[:, j, :], in0=l_sb[:, j, :], scalar=c_j[:, j:j + 1], in1=mr[:], op0=ALU.add, op1=ALU.subtract)

        z_wide = {}

        def widen(g, t, eng):
            if g not in z_wide:
                z_wide[g] = work.tile([P, T, P_OUT], BF16, name="z_wide", tag="late%d" % g, bufs=1)
            src = z_in[g][:, P_OUT * t:P_OUT * (t + 1)].bitcast(FP8)
            sc = zs[:, T * g + t:T * g + t + 1]
            if eng == "V":
                nc.vector.tensor_scalar(out=z_wide[g][:, t, :], in0=src, scalar1=sc, scalar2=None, op0=ALU.mult)
            else:
                nc.scalar.activation(z_wide[g][:, t, :], src, ACT.Copy, scale=sc)

        def z_group(g, n):
            flat = work.tile([P, R * T], BF16, name="zg", align_bytes=64, bufs=2)
            zg = flat[:].rearrange("p (c t) -> p c t", t=T)
            banks["zg", g, n] = flat
            nc.vector.tensor_copy(
                out=zg.rearrange("p (c i) t -> p c t i", i=4),
                in_=z_wide[g][:, :, R * n:R * (n + 1)].rearrange("p t (c i) -> p c t i", i=4),
            )

        def z_quant(g, n):
            quant(("z", n, g), banks["zg", g, n][:])

        def a_make(g, lo, hi):
            h, w = lo // R, hi - lo
            if (h, g) not in grouped:
                grouped[h, g] = work.tile([P, R * T], BF16, name="grouped", align_bytes=64, bufs=8)
                codes["a", h, g] = keep.tile([P, R], U32, name="c_a%d%d" % (h, g), align_bytes=64)
                scales["a", h, g] = keep.tile([P, R], U8, name="s_a%d%d" % (h, g), align_bytes=64)
            at = lo - R * h
            nc.vector.tensor_tensor(
                out=grouped[h, g][:, T * at:T * (at + w)].rearrange("p (c i t) -> p c t i", i=4, t=T),
                in0=l_sb[:, T * g:T * (g + 1), lo:hi].rearrange("p t (c i) -> p c t i", i=4),
                in1=k_sb[g][:, :, lo:hi].rearrange("p t (c i) -> p c t i", i=4),
                op=ALU.mult,
            )

        def a_quant(g, lo, hi):
            h = lo // R
            at, to = lo - R * h, hi - R * h
            nc.vector.quantize_mx(out=codes["a", h, g][:, at:to].bitcast(FP8X4), scales=scales["a", h, g][:, at:to], in_=grouped[h, g][:, T * at:T * to])

        out_rows = out.rearrange("(h m t) p -> h t m p", m=P, t=T)
        staged = {}

        def o_mm(tile, n, slot):
            banks["o", tile, n] = mm("a", "z", tile // T, n, tile % T, 2, slot)

        def o_out(tile, n, eng):
            bank = banks["o", tile, n]
            if tile not in staged:
                staged[tile] = work.tile([P, P_OUT], F32, name="wide32", bufs=4)
                count[tile] = 0
            cols = slice(R * n, R * (n + 1))
            dst = staged[tile][:, cols]
            if eng == "V":
                nc.vector.tensor_scalar(out=dst, in0=bank[:], scalar1=M ** -0.5, scalar2=None, op0=ALU.mult)
            else:
                nc.scalar.activation(dst, bank[:], ACT.Copy, scale=M ** -0.5)
            count[tile] += 1
            if tile >= 6:
                nc.sync.dma_start(out=out_rows[tile // T, tile % T][:, cols], in_=dst)
            elif count[tile] == 2:
                nc.sync.dma_start(out=out_rows[tile // T, tile % T], in_=staged[tile][:])

        count = {}

        r_finish()
        turn("v", 0, 0, 0, 0)
        turn("v", 0, 0, 1, 1)
        empty("v", 0, 0, 0, "V")
        turn("y", 0, 0, 0, 2)
        empty("v", 0, 0, 1, "V")
        turn("y", 0, 0, 1, 3)
        empty("y", 0, 0, 0, "S")
        q("v", 0, 0)
        empty("y", 0, 0, 1, "S")
        turn("v", 1, 0, 0, 4)
        turn("v", 1, 0, 1, 5)
        q("y", 0, 0)
        empty("v", 1, 0, 0, "S")
        turn("y", 1, 0, 0, 0)
        empty("v", 1, 0, 1, "V")
        turn("y", 1, 0, 1, 1)
        empty("y", 1, 0, 0, "S")
        widen(0, 2, "V")
        l_mm(2, 0, 2)
        empty("y", 1, 0, 1, "S")
        l_mm(3, 0, 3)
        q("v", 1, 0)
        l_mm(0, 0, 4)
        l_exp(2, 0)
        l_mm(1, 0, 5)
        q("y", 1, 0)
        turn("u", 0, 1, 0, 0)
        l_exp(0, 0)
        widen(0, 0, "V")
        l_mm(6, 0, 1)
        l_exp(1, 0)
        l_mm(0, 1, 2)
        widen(0, 3, "V")
        l_mm(1, 1, 4)
        l_exp(3, 0)
        l_mm(2, 1, 5)
        add_pair(0, 0)
        l_exp(0, 1)
        l_mm(3, 1, 3)
        widen(1, 2, "V")
        row_means_mm(0, 0, 0)
        l_exp(2, 1)
        widen(1, 3, "V")
        l_exp(3, 1)
        add_pair(1, 0)
        l_mm(7, 0, 2)
        l_exp(1, 1)
        l_mm(4, 1, 5)
        widen(1, 0, "V")
        l_mm(5, 1, 3)
        widen(1, 1, "S")
        row_means_mm(1, 0, 1)
        add_pair(0, 1)
        add_pair(1, 1)
        l_exp(4, 1)
        row_means_mm(0, 1, 0)
        z_group(1, 0)
        l_exp(5, 1)
        l_exp(6, 0)
        l_mm(4, 0, 4)
        add_pair(2, 1)
        l_mm(5, 0, 5)
        l_exp(7, 0)
        l_mm(6, 1, 3)
        z_quant(1, 0)
        l_mm(7, 1, 1)
        row_means_mm(1, 1, 1)
        l_exp(6, 1)
        add_pair(3, 0)
        l_exp(7, 1)
        z_group(1, 1)
        row_means_mm(2, 1, 2)
        l_exp(4, 0)
        l_exp(5, 0)
        col_sums()
        add_pair(3, 1)
        turn("u", 0, 1, 1, 2)
        widen(0, 1, "S")
        z_quant(1, 1)
        row_means_mm(3, 1, 3)
        add_pair(2, 0)
        empty("u", 0, 1, 1, "S")
        z_group(0, 0)
        row_means_mm(2, 0, 2)
        empty("u", 0, 1, 0, "S")
        row_means_out(1)
        q("u", 0, 1)
        row_means_mm(3, 0, 3)
        z_quant(0, 0)
        z_group(0, 1)
        turn("x", 1, 1, 0, 3)
        row_means_out(0)
        turn("x", 1, 1, 1, 1)
        empty("x", 1, 1, 0, "S")
        col_terms()
        turn("x", 0, 1, 0, 4)
        z_quant(0, 1)
        empty("x", 1, 1, 1, "S")
        turn("x", 0, 1, 1, 5)
        centre(7)
        empty("x", 0, 1, 0, "S")
        turn("x", 0, 0, 0, 2)
        empty("x", 0, 1, 1, "S")
        turn("x", 0, 0, 1, 0)
        centre(4)
        empty("x", 0, 0, 0, "S")
        turn("u", 1, 1, 0, 3)
        empty("x", 0, 0, 1, "S")
        turn("u", 1, 1, 1, 1)
        q("x", 1, 1)
        empty("u", 1, 1, 0, "S")
        turn("u", 0, 0, 0, 4)
        turn("u", 0, 0, 1, 5)
        q("x", 0, 0)
        empty("u", 1, 1, 1, "S")
        turn("x", 1, 0, 0, 2)
        empty("u", 0, 0, 0, "S")
        q("x", 0, 1)
        turn("x", 1, 0, 1, 0)
        empty("u", 0, 0, 1, "S")
        q("u", 1, 1)
        turn("u", 1, 0, 0, 3)
        empty("x", 1, 0, 0, "S")
        q("u", 0, 0)
        turn("u", 1, 0, 1, 1)
        empty("x", 1, 0, 1, "S")
        centre(5)
        k_mm(0, 0, 4)
        empty("u", 1, 0, 1, "S")
        k_mm(1, 0, 5)
        empty("u", 1, 0, 0, "S")
        q("x", 1, 0)
        k_mm(2, 0, 2)
        k_exp(0, 0)
        q("u", 1, 0)
        k_mm(3, 0, 0)
        k_exp(1, 0)
        centre(3)
        k_mm(0, 1, 1)
        k_exp(2, 0)
        k_mm(4, 0, 3)
        k_exp(3, 0)
        centre(1)
        k_mm(5, 0, 4)
        k_exp(4, 0)
        k_mm(1, 1, 5)
        k_exp(5, 0)
        k_mm(6, 0, 2)
        centre(6)
        k_exp(0, 1)
        k_mm(7, 0, 0)
        k_exp(6, 0)
        k_mm(4, 1, 3)
        centre(0)
        k_exp(7, 0)
        k_mm(5, 1, 4)
        k_exp(1, 1)
        k_mm(6, 1, 1)
        centre(2)
        k_mm(7, 1, 2)
        k_exp(4, 1)
        k_mm(2, 1, 0)
        k_exp(6, 1)
        a_make(1, 256, 512)
        k_mm(3, 1, 5)
        k_exp(7, 1)
        k_exp(2, 1)
        a_make(0, 256, 512)
        k_exp(3, 1)
        k_exp(5, 1)
        a_quant(1, 256, 512)
        a_quant(0, 256, 512)
        a_make(1, 896, 1024)
        o_mm(2, 0, 3)
        a_make(0, 896, 1024)
        o_mm(2, 1, 1)
        o_out(2, 0, "S")
        a_quant(1, 896, 1024)
        o_mm(3, 0, 2)
        a_make(0, 0, 256)
        o_out(2, 1, "S")
        o_mm(3, 1, 0)
        o_out(3, 0, "S")
        a_quant(0, 896, 1024)
        o_out(3, 1, "S")
        a_make(1, 0, 256)
        o_mm(7, 0, 5)
        o_mm(7, 1, 4)
        o_out(7, 0, "S")
        a_quant(0, 0, 256)
        a_quant(1, 0, 256)
        o_out(7, 1, "S")
        a_make(0, 512, 768)
        o_mm(1, 0, 3)
        o_mm(1, 1, 1)
        o_out(1, 0, "S")
        a_make(1, 512, 768)
        o_mm(0, 0, 2)
        o_out(1, 1, "S")
        o_mm(0, 1, 0)
        o_out(0, 0, "S")
        a_quant(0, 512, 768)
        a_quant(1, 512, 768)
        o_out(0, 1, "S")
        a_make(1, 768, 896)
        o_mm(5, 0, 5)
        a_make(0, 768, 896)
        o_mm(5, 1, 4)
        o_out(5, 0, "S")
        a_quant(1, 768, 896)
        o_mm(4, 0, 3)
        a_quant(0, 768, 896)
        o_out(5, 1, "S")
        o_mm(4, 1, 1)
        o_out(4, 0, "S")
        o_mm(6, 0, 2)
        o_out(4, 1, "V")
        o_mm(6, 1, 0)
        o_out(6, 0, "V")
        o_out(6, 1, "S")
